import numpy as np, ml_dtypes
CORES = [3,7,11,15,131,135,139,143]
N = 8
import mx_ref
NC, K = 256, 2
CNT = [[0,48,0,56,16,32,0,104],[48,64,16,40,0,0,88,0],[0,0,0,48,120,40,40,8],[80,32,56,0,16,56,0,16],[0,16,48,0,32,64,96,0],[40,64,32,0,24,48,0,48],[40,32,48,104,0,0,32,0],[48,0,56,8,48,16,0,80]]
OFF = [[sum(c[:e]) for e in range(N + 1)] for c in CNT]
BF = ml_dtypes.bfloat16
def setup_inputs(rng):
    def f(*shape):
        return mx_ref.flush((rng.standard_normal(shape, dtype=np.float32) * np.exp2(rng.integers(-2, 3, shape[:-1] + (1,)))).astype(BF))
    return {"x": f(N, 128, 4 * NC), "w": f(N, 128, 512)}
def setup_inputs_blocks(rng):
    d = setup_inputs(rng)
    for k in ("x", "w"): d[k] = mx_ref.spread(d[k], rng, 4)
    return d
def setup_inputs_wide(rng):
    d = setup_inputs(rng)
    for k in ("x", "w"): d[k] = mx_ref.flush((d[k].astype(np.float32) * np.exp2(rng.integers(-8, 9, (N, 1, 1))).astype(np.float32)).astype(BF))
    return d
def setup_inputs_zeros(rng):
    d = setup_inputs(rng); v = d["x"].reshape(N, 128, -1, 4).copy()
    v[np.broadcast_to((rng.random((N, 1, v.shape[2], 1)) < 0.33), v.shape)] = 0
    d["x"] = v.reshape(d["x"].shape)
    return d
def reference(x, w):
    y = np.zeros((N, 128, K * NC), np.float32)
    for e in range(N):
        t = np.concatenate([x[j][:, 4 * OFF[j][(e - k) % N]:4 * OFF[j][(e - k) % N + 1]] for k in range(K) for j in range(N)], axis=1)
        y[e] = mx_ref.matmul(mx_ref.quantize(w[e]), mx_ref.quantize(t))
    return {"y": y}

@@ -1,0 +1,296 @@
+from concourse.bass import DstId, RemoteDMATransfer
+from concourse.mybir import dt, ActivationFunctionType
+
+LAND = 1280
+SCRATCH = {
+    "xt": ("sbuf", [128, 4 * 512], "bfloat16"),
+    "wt": ("sbuf", [128, 512], "bfloat16"),
+    "qa": ("sbuf", [128, 256], "float8_e4m3fn_x4"),
+    "pa": ("sbuf", [128, 256], "uint8"),
+    "qb": ("sbuf", [128, 512], "float8_e4m3fn_x4"),
+    "pb": ("sbuf", [128, 512], "uint8"),
+    "qw": ("sbuf", [128, 128], "float8_e4m3fn_x4"),
+    "pw": ("sbuf", [128, 128], "uint8"),
+    "ql": ("sbuf", [128, LAND], "float8_e4m3fn_x4"),
+    "pl": ("sbuf", [128, LAND], "uint8"),
+    "ys": ("sbuf", [128, 512], "float32"),
+    "ps": ("psum", [128, 5 * 512], "float32"),
+}
+SEMAPHORES = ["xa", "xb", "wl", "qad", "qbd", "qwd", "sent", "hc", "hs", "loc", "rel",
+              "m0", "m1", "m2", "m3", "m4", "c0", "c1", "c2", "c3", "c4", "st"]
+LEAST = 128
+
+
+def bits(m):
+    return [i for i in range(m.bit_length()) if m >> i & 1]
+
+
+def as_mask(engines):
+    return sum(1 << i for i in engines)
+
+
+def span(pos, fs):
+    r = [pos[f] for f in fs if pos[f][1] > pos[f][0]]
+    return (min(a for a, b in r), max(b for a, b in r)) if r else None
+
+
+def plan(T, topo):
+    cores, cnt = list(T.cores), T.tables["CNT"]
+    n = len(cores)
+    mine = [[r for r in range(n) if topo.host(cores[r]) == topo.host(cores[j])] for j in range(n)]
+    seq, na, posa, lob, nb, posb = [], [], [], [], [], []
+    for j in range(n):
+        s, h, c = mine[j][0], len(mine[j]), cnt[j]
+        off = [sum(c[:f]) for f in range(n + 1)]
+        far = [(s + h - 1 + i) % n for i in range(n - h + 1)]
+        near = [(s - 1 + i) % n for i in range(h + 1)]
+        seq.append([x for f in far + near[1:] for x in range(off[f], off[f + 1])])
+        at, p = 0, {}
+        for f in far:
+            p[f] = (at, at + c[f])
+            at += c[f]
+        posa.append(p)
+        na.append(at)
+        first = at - c[near[0]]
+        lo = min(first, len(seq[j]) - LEAST)
+        lob.append(lo)
+        nb.append(len(seq[j]) - lo)
+        at, p = first - lo, {}
+        for f in near:
+            p[f] = (at, at + c[f])
+            at += c[f]
+        posb.append(p)
+
+    def slots(pos, dests):
+        need = {e: span(pos, [(e - 1) % n, e]) for e in dests}
+        need = {e: v for e, v in need.items() if v}
+        return need, max([b - a for a, b in need.values()] + [0])
+
+    local = [slots(posb[j], [e for e in mine[j] if e != j]) for j in range(n)]
+
+    cand = [[r for r in range(n) if r not in mine[j] and topo.same_plane(cores[j], cores[r])] for j in range(n)]
+    fwd = {(j, r): slots(posa[j], [e for e in mine[r] if e != r]) for j in range(n) for r in cand[j]}
+    relay = {}
+    for group in sorted(set(tuple(m) for m in mine)):
+        best = []
+
+        def search(k, chosen):
+            if k == len(group):
+                cost = [na[j] + 2 * fwd[j, r][1] for j, r in chosen.items()]
+                cross = sum(na[j] for j, r in chosen.items() if topo.die(cores[j]) != topo.die(cores[r]))
+                best.append(((max(cost), sum(cost), cross), sorted(chosen.items())))
+                return
+            for r in cand[group[k]]:
+                if r not in chosen.values():
+                    search(k + 1, {**chosen, group[k]: r})
+        search(0, {})
+        for j, r in min(best)[1]:
+            relay[j] = r
+    source = {r: j for j, r in relay.items()}
+
+    place = []
+    for e in range(n):
+        at, p = 0, {}
+        for j in mine[e]:
+            if j != e and e in local[j][0]:
+                p["local", j] = at
+                at += local[j][1]
+        p["hop"] = at
+        at += na[source[e]]
+        for r in mine[e]:
+            if r != e and e in fwd[source[r], r][0]:
+                p["relay", source[r]] = at
+                at += fwd[source[r], r][1]
+        assert at <= LAND
+        place.append(p)
+    return dict(cores=cores, cnt=cnt, n=n, mine=mine, seq=seq, na=na, posa=posa, lob=lob, nb=nb, posb=posb,
+                local=local, fwd=fwd, relay=relay, source=source, place=place)
+
+
+def rank_program(g, core, T, topo):
+    me = T.rank_of(core)
+    if me is None:
+        return
+    P = plan(T, topo)
+    cores, cnt, n, mine = P["cores"], P["cnt"], P["n"], P["mine"]
+    S = T.sem
+    total = sum(cnt[me])
+    src = P["source"][me]
+    place = P["place"][me]
+
+    seq, na = P["seq"][me], P["na"][me]
+    wa = max(na, LEAST)
+
+    def pieces(lo, hi):
+        out, a = [], lo
+        for i in range(lo + 1, hi + 1):
+            if i == hi or seq[i] != seq[i - 1] + 1:
+                out.append((a, i))
+                a = i
+        return out
+
+    def load(q, a, b, sem):
+        q.dma_start(T.xt[:, 4 * a:4 * b], T.x[:, 4 * seq[a]:4 * (seq[b - 1] + 1)]).then_inc(sem, 16)
+
+    first, rest = pieces(0, wa), pieces(wa, len(seq))
+    for i, (a, b) in enumerate(first):
+        load([g.sync, g.scalar][i % 2], a, b, S.xa)
+    for a, b in rest:
+        load(g.sync, a, b, S.xb)
+    g.sync.dma_start(T.wt[:, :], T.w[:, :]).then_inc(S.wl, 16)
+
+    lob, nb = P["lob"][me], P["nb"][me]
+    g.vector.wait_ge(S.xa, 16 * len(first))
+    g.vector.quantize_mx(T.qa[:, 0:wa], T.pa[:, 0:wa], T.xt[:, 0:4 * wa]).then_inc(S.qad, 1)
+    if rest:
+        g.vector.wait_ge(S.xb, 16 * len(rest))
+    g.vector.quantize_mx(T.qb[:, 0:nb], T.pb[:, 0:nb], T.xt[:, 4 * lob:4 * (lob + nb)]).then_inc(S.qbd, 1)
+    g.vector.wait_ge(S.wl, 16)
+    g.vector.quantize_mx(T.qw[:, :], T.pw[:, :], T.wt[:, :]).then_inc(S.qwd, 1)
+
+    sent = [0]
+
+    def engines(sender, dests):
+        here = cores[sender]
+        on = [e for e in dests if topo.host(cores[e]) == topo.host(here) and topo.chip(cores[e]) == topo.chip(here)]
+        off = [e for e in dests if e not in on]
+        leave = bits(topo.mask(here, cores[P["relay"][sender]]))
+        k = len(leave)
+        while k * len(off) > len(leave):
+            k //= 2
+        out = {e: leave[i * k:(i + 1) * k] for i, e in enumerate(off)}
+        for e in on:
+            out[e] = [i for i in bits(topo.mask(here, cores[e])) if i not in leave][::2]
+        assert len(on) <= 1
+        return out
+
+    def send(buf, is_codes, need, w, base, limit, key, sem):
+        eng = engines(me, sorted(need))
+        tr = []
+        for e in sorted(need):
+            a = base + min(need[e][0], limit - w)
+            d = P["place"][e][key]
+            s_ap, d_ap = buf[:, a:a + w], (T.ql if is_codes else T.pl)[:, d:d + w]
+            if is_codes:
+                s_ap, d_ap = s_ap.bitcast(dt.uint8), d_ap.bitcast(dt.uint8)
+            rid, pid = topo.addr(cores[e], core)
+            tr.append(RemoteDMATransfer(dst_ids=[DstId(rid=rid, pnc=pid)], dma_engine_mask=as_mask(eng[e]), remote_sem=sem,
+                                        srcs=[s_ap], dsts=[d_ap]))
+            sent[0] += len(eng[e])
+        g.remote_dma_fused(tr, local_sem=S.sent)
+
+    to = P["relay"][me]
+    rid, pid = topo.addr(cores[to], core)
+    hop_mask = topo.mask(core, cores[to])
+    d = P["place"][to]["hop"]
+    g.wait_ge(S.qad, 1)
+    g.remote_dma(T.ql[:, d:d + na].bitcast(dt.uint8), T.qa[:, 0:na].bitcast(dt.uint8), S.hc, S.sent, pid, rid, hop_mask)
+    g.remote_dma(T.pl[:, d:d + na], T.pa[:, 0:na], S.hs, S.sent, pid, rid, hop_mask)
+    sent[0] += 2 * len(bits(hop_mask))
+
+    need, w = P["local"][me]
+    g.wait_ge(S.qbd, 1)
+    send(T.qb, True, need, w, 0, nb, ("local", me), S.loc)
+    send(T.pb, False, need, w, 0, nb, ("local", me), S.loc)
+
+    hop_inc = len(bits(topo.mask(cores[src], core)))
+    need, w = P["fwd"][src, me]
+    hop, hop_n = place["hop"], P["na"][src]
+    g.wait_ge(S.hc, hop_inc)
+    send(T.ql, True, need, w, hop, hop_n, ("relay", src), S.rel)
+    g.wait_ge(S.hs, hop_inc)
+    send(T.pl, False, need, w, hop, hop_n, ("relay", src), S.rel)
+    g.wait_ge(S.sent, sent[0])
+
+    prev = (me - 1) % n
+    yat = {}
+    for half, f in enumerate((me, prev)):
+        at = half * total
+        for j in range(n):
+            yat[half, j] = at
+            at += cnt[j][f]
+
+    def runs(j, pos, shift):
+        return [(yat[half, j], shift + pos[f][0], cnt[j][f]) for half, f in enumerate((me, prev)) if cnt[j][f]]
+
+    own = runs(me, P["posb"][me], 0)
+    loc, loc_inc = [], 0
+    for j in mine[me]:
+        if ("local", j) in place:
+            nd, w = P["local"][j]
+            loc += runs(j, P["posb"][j], place["local", j] - min(nd[me][0], P["nb"][j] - w))
+            loc_inc += 2 * len(engines(j, sorted(nd))[me])
+    hopr = runs(src, P["posa"][src], hop)
+    rel, rel_inc = [], 0
+    for r in mine[me]:
+        j = P["source"][r]
+        if ("relay", j) in place:
+            nd, w = P["fwd"][j, r]
+            rel.append(runs(j, P["posa"][j], place["relay", j] - min(nd[me][0], P["na"][j] - w)))
+            rel_inc += 2 * len(engines(r, sorted(nd))[me])
+
+    def work(rs):
+        return sum(max(c, 64) for x in rs for _, _, c in x)
+    k = min(range(len(rel) + 1), key=lambda k: max(work(rel[:k]), work(rel[k:])))
+    rel_v, rel_s = [x for y in rel[:k] for x in y], [x for y in rel[k:] for x in y]
+
+    groups = [(T.qb, T.pb, own, nb), (T.ql, T.pl, loc, hop), (T.ql, T.pl, hopr, hop + hop_n),
+              (T.ql, T.pl, rel_v, LAND), (T.ql, T.pl, rel_s, LAND)]
+    lows = []
+    for b, (q, p, rs, end) in enumerate(groups):
+        if b == 0:
+            g.tensor.wait_ge(S.qbd, 1)
+            g.tensor.wait_ge(S.qwd, 1)
+        elif b == 1 and loc_inc:
+            g.tensor.wait_ge(S.loc, loc_inc)
+        elif b == 2:
+            g.tensor.wait_ge(S.hc, hop_inc)
+            g.tensor.wait_ge(S.hs, hop_inc)
+        elif b == 3 and rel_inc:
+            g.tensor.wait_ge(S.rel, rel_inc)
+        lows.append(0)
+        if not rs:
+            continue
+        lo, hi = min(a for _, a, c in rs), max(a + c for _, a, c in rs)
+        lo = max(0, min(lo, hi - LEAST))
+        hi = max(hi, lo + LEAST)
+        assert hi <= end and hi - lo <= 512
+        lows[b] = lo
+        g.tensor.matmul_mx(T.ps[:, 512 * b:512 * b + hi - lo], T.qw[:, :], T.pw[:, :], q[:, lo:hi], p[:, lo:hi],
+                           True, True).then_inc(S["m%d" % b], 1)
+
+    def pick(b):
+        rs = groups[b][2]
+        if not rs:
+            return
+        q = g.scalar if b in (1, 4) else g.vector
+        q.wait_ge(S["m%d" % b], 1)
+        for y, a, c in rs:
+            o, i = T.ys[:, y:y + c], T.ps[:, 512 * b + a - lows[b]:512 * b + a - lows[b] + c]
+            if b in (1, 4):
+                q.activation(o, i, ActivationFunctionType.Copy).then_inc(S["c%d" % b], 1)
+            else:
+                q.tensor_copy(o, i).then_inc(S["c%d" % b], 1)
+
+    def store(q, half, js, banks):
+        for b in banks:
+            if groups[b][2]:
+                q.wait_ge(S["c%d" % b], len(groups[b][2]))
+        lo = yat[half, js[0]]
+        hi = yat[half, js[-1]] + cnt[js[-1]][(me, prev)[half]]
+        if hi > lo:
+            q.dma_start(T.y[:, lo:hi], T.ys[:, lo:hi]).then_inc(S.st, 16)
+            return 1
+        return 0
+
+    far = [j for j in range(n) if j not in mine[me]]
+    pick(0)
+    pick(2)
+    pick(3)
+    pick(1)
+    k = store(g.scalar, 1, mine[me], (0, 1))
+    pick(4)
+    k += store(g.scalar, 1, far, (2, 3, 4))
+    k += store(g.sync, 0, mine[me], (0, 1))
+    k += store(g.sync, 0, far, (2, 3, 4))
+    g.sync.wait_ge(S.st, 16 * k)

@@ -1,23 +1,21 @@
 from concourse.bass import DstId, RemoteDMATransfer
 from concourse.mybir import dt, ActivationFunctionType
 
-LAND = 1280
+TILE, LAND = 512, 2048
 SCRATCH = {
-    "xt": ("sbuf", [128, 4 * 512], "bfloat16"),
+    "xt": ("sbuf", [128, 4 * TILE], "bfloat16"),
     "wt": ("sbuf", [128, 512], "bfloat16"),
-    "qa": ("sbuf", [128, 256], "float8_e4m3fn_x4"),
-    "pa": ("sbuf", [128, 256], "uint8"),
-    "qb": ("sbuf", [128, 512], "float8_e4m3fn_x4"),
-    "pb": ("sbuf", [128, 512], "uint8"),
+    "q": ("sbuf", [128, TILE], "float8_e4m3fn_x4"),
+    "p": ("sbuf", [128, TILE], "uint8"),
     "qw": ("sbuf", [128, 128], "float8_e4m3fn_x4"),
     "pw": ("sbuf", [128, 128], "uint8"),
     "ql": ("sbuf", [128, LAND], "float8_e4m3fn_x4"),
     "pl": ("sbuf", [128, LAND], "uint8"),
     "ys": ("sbuf", [128, 512], "float32"),
-    "ps": ("psum", [128, 5 * 512], "float32"),
+    "ps": ("psum", [128, 8 * 512], "float32"),
 }
-SEMAPHORES = ["xa", "xb", "wl", "qad", "qbd", "qwd", "sent", "hc", "hs", "loc", "rel",
-              "m0", "m1", "m2", "m3", "m4", "c0", "c1", "c2", "c3", "c4", "st"]
+SEMAPHORES = (["xa", "xb", "wl", "qad", "qbd", "qwd", "sent", "hop", "direct", "shared", "loc", "st"] + ["rel%d" % i for i in range(8)]
+              + ["m%d" % b for b in range(8)] + ["c%s%d%s" % (a, h, e) for a in "el" for h in (0, 1) for e in "vs"])
 LEAST = 128
 
 
@@ -30,81 +28,204 @@ def as_mask(engines):
 
 
 def span(pos, fs):
-    r = [pos[f] for f in fs if pos[f][1] > pos[f][0]]
-    return (min(a for a, b in r), max(b for a, b in r)) if r else None
+    r = sorted(pos[f] for f in fs if pos[f][1] > pos[f][0])
+    if not r:
+        return None
+    assert all(a[1] == b[0] for a, b in zip(r, r[1:]))
+    return r[0][0], r[-1][1]
+
+
+def spans(pos, wants):
+    need = {e: span(pos, fs) for e, fs in wants.items()}
+    return {e: r for e, r in need.items() if r}
+
+
+def positions(order, c, at=0):
+    pos = {}
+    for f in order:
+        pos[f] = (at, at + c[f])
+        at += c[f]
+    return pos
+
+
+def width(need):
+    return max(b - a for a, b in need.values())
+
+
+def both(x, y):
+    return (max(x[0], y[0]), min(x[1], y[1]))
+
+
+def orders(items):
+    if not items:
+        yield []
+    for i, x in enumerate(items):
+        for rest in orders(items[:i] + items[i + 1:]):
+            yield [x] + rest
+
+
+def arrange(nloc, items, seek, turn, hop):
+    for order in orders(["local"] + sorted(items)):
+        at, base, whole, loc = 0, {}, {}, 0
+        for j in order:
+            if j == "local":
+                loc = at
+                whole[j] = (at, at + nloc)
+                at += nloc
+            else:
+                c, p = items[j]
+                lo, hi = min(c[0], p[0]), max(c[1], p[1])
+                base[j] = at - lo
+                f = both(c, p)
+                whole[j] = (base[j] + f[0], base[j] + max(f))
+                at += hi - lo
+        here, windows, taken, todo = {"local", hop}, {}, [], list(turn)
+
+        def window(r, have):
+            lo = hi = None
+            for j in order:
+                a, b = whole[j]
+                if j in have and b > a:
+                    lo, hi = (lo, b) if hi == a else (a, b)
+                    if lo <= r[0] and r[1] <= hi:
+                        end = hi
+                        for i in order[order.index(j) + 1:]:
+                            if i not in have or whole[i][0] != end or whole[i][1] == end:
+                                break
+                            end = whole[i][1]
+                        if end - lo < LEAST:
+                            return None
+                        a = max(lo, min(r[0], r[1] - LEAST))
+                        return a, max(r[1], a + LEAST)
+            return None
+
+        def take(j):
+            got = [window((base[j] + r[0], base[j] + r[1]), here | {j}) for r in seek[j]]
+            if None in got:
+                return False
+            here.add(j)
+            taken.append(j)
+            windows.update({(j, r): w for r, w in zip(seek[j], got)})
+            return True
+
+        ok, waiting = True, True
+        while ok and (todo or waiting):
+            if waiting and take(hop):
+                waiting = False
+            elif todo and not (waiting and len(todo) == 1):
+                ok = take(todo.pop(0))
+            else:
+                ok = False
+        if ok:
+            return loc, base, at, taken, windows
+    assert False, "no order of the sources gives every run a window"
 
 
 def plan(T, topo):
     cores, cnt = list(T.cores), T.tables["CNT"]
     n = len(cores)
     mine = [[r for r in range(n) if topo.host(cores[r]) == topo.host(cores[j])] for j in range(n)]
-    seq, na, posa, lob, nb, posb = [], [], [], [], [], []
+    chipmates = [[r for r in mine[j] if topo.chip(cores[r]) == topo.chip(cores[j])] for j in range(n)]
+
+    seq, na, posa, posb, split = [], [], [], [], []
     for j in range(n):
         s, h, c = mine[j][0], len(mine[j]), cnt[j]
         off = [sum(c[:f]) for f in range(n + 1)]
         far = [(s + h - 1 + i) % n for i in range(n - h + 1)]
         near = [(s - 1 + i) % n for i in range(h + 1)]
-        seq.append([x for f in far + near[1:] for x in range(off[f], off[f + 1])])
-        at, p = 0, {}
-        for f in far:
-            p[f] = (at, at + c[f])
-            at += c[f]
-        posa.append(p)
-        na.append(at)
-        first = at - c[near[0]]
-        lo = min(first, len(seq[j]) - LEAST)
-        lob.append(lo)
-        nb.append(len(seq[j]) - lo)
-        at, p = first - lo, {}
-        for f in near:
-            p[f] = (at, at + c[f])
-            at += c[f]
-        posb.append(p)
+        q = [x for f in far + near[1:] for x in range(off[f], off[f + 1])]
+        na.append(sum(c[f] for f in far))
+        posa.append(positions(far, c))
+        posb.append(positions(near, c, posa[j][near[0]][0]))
+        split.append(max(na[j], LEAST))
+        more = q[-1] + 1
+        while len(q) < split[j] + LEAST:
+            q.append(more % sum(c))
+            more += 1
+        seq.append(q)
 
-    def slots(pos, dests):
-        need = {e: span(pos, [(e - 1) % n, e]) for e in dests}
-        need = {e: v for e, v in need.items() if v}
-        return need, max([b - a for a, b in need.values()] + [0])
+    def wants(dests):
+        return {e: [(e - 1) % n, e] for e in dests}
 
-    local = [slots(posb[j], [e for e in mine[j] if e != j]) for j in range(n)]
+    local = [spans(posb[j], wants([e for e in mine[j] if e != j])) for j in range(n)]
 
     cand = [[r for r in range(n) if r not in mine[j] and topo.same_plane(cores[j], cores[r])] for j in range(n)]
-    fwd = {(j, r): slots(posa[j], [e for e in mine[r] if e != r]) for j in range(n) for r in cand[j]}
+    fwd = {(j, r): spans(posa[j], wants([e for e in mine[r] if e != r])) for j in range(n) for r in cand[j]}
+    work = {(j, r): na[j] + width(v) * len([e for e in v if e not in chipmates[r]]) for (j, r), v in fwd.items()}
     relay = {}
     for group in sorted(set(tuple(m) for m in mine)):
-        best = []
+        tried = []
 
         def search(k, chosen):
             if k == len(group):
-                cost = [na[j] + 2 * fwd[j, r][1] for j, r in chosen.items()]
+                cost = [work[j, r] for j, r in chosen.items()]
                 cross = sum(na[j] for j, r in chosen.items() if topo.die(cores[j]) != topo.die(cores[r]))
-                best.append(((max(cost), sum(cost), cross), sorted(chosen.items())))
+                tried.append(((max(cost), sum(cost), cross), sorted(chosen.items())))
                 return
             for r in cand[group[k]]:
                 if r not in chosen.values():
                     search(k + 1, {**chosen, group[k]: r})
         search(0, {})
-        for j, r in min(best)[1]:
+        for j, r in min(tried)[1]:
             relay[j] = r
     source = {r: j for j, r in relay.items()}
+    fwd = [fwd[j, relay[j]] for j in range(n)]
+    work = [work[j, relay[j]] for j in range(n)]
 
-    place = []
+    direct, union = [[] for _ in range(n)], [{} for _ in range(n)]
+    for r in range(n):
+        i = chipmates[r].index(r)
+        for j in [j for j in range(n) if j not in mine[r]][i::len(chipmates[r])]:
+            fs = sorted(set(f for e in chipmates[r] for f in ((e - 1) % n, e)))
+            if span(posa[j], fs):
+                union[j][r] = span(posa[j], fs)
+                direct[r].append(j)
+
+    place, taken, windows = [], [], []
     for e in range(n):
-        at, p = 0, {}
+        at, p, items, seek = 0, {}, {}, {}
         for j in mine[e]:
-            if j != e and e in local[j][0]:
-                p["local", j] = at
-                at += local[j][1]
-        p["hop"] = at
-        at += na[source[e]]
-        for r in mine[e]:
-            if r != e and e in fwd[source[r], r][0]:
-                p["relay", source[r]] = at
-                at += fwd[source[r], r][1]
-        assert at <= LAND
+            if e in local[j]:
+                w = width(local[j])
+                p["local", j] = (at, min(local[j][e][0], len(seq[j]) - w), w)
+                at += w
+        turn = sorted([source[r] for r in mine[e] if r != e and e in fwd[source[r]]], key=lambda j: (work[j], j))
+        for r in chipmates[e]:
+            for j in direct[r]:
+                if r == e or e in fwd[j] or source[e] == j:
+                    w = width(union[j])
+                    a = min(union[j][r][0], na[j] - w)
+                    items[j] = ((a, a), (a, a + w))
+        for j in set(turn + [source[e]]):
+            need = span(posa[j], [(e - 1) % n, e])
+            planes = items[j][1] if j in items else (0, 0)
+            if j == source[e]:
+                codes = (0, na[j])
+            else:
+                w = width(fwd[j])
+                starts = range(max(0, need[1] - w), min(need[0], na[j] - w) + 1, 2)
+                a = max(starts, key=lambda a: (both((a, a + w), planes)[1] - both((a, a + w), planes)[0], a))
+                codes = (a, a + w)
+            items[j] = (codes, planes)
+            if not need:
+                seek[j] = []
+            elif turn and j == turn[-1]:
+                seek[j] = [posa[j][f] for f in (e, (e - 1) % n) if cnt[j][f]]
+            else:
+                seek[j] = [need]
+        loc, base, end, order, wins = arrange(at, items, seek, turn, source[e])
+        assert end <= LAND
+        p = {k: (loc + d, a, w) for k, (d, a, w) in p.items()}
+        for j, (codes, planes) in items.items():
+            p["codes", j] = (base[j] + codes[0], codes[0], codes[1] - codes[0])
+            p["plane", j] = (base[j] + planes[0], planes[0], planes[1] - planes[0])
+        p["base"], p["loc"] = base, (loc, loc + at)
         place.append(p)
-    return dict(cores=cores, cnt=cnt, n=n, mine=mine, seq=seq, na=na, posa=posa, lob=lob, nb=nb, posb=posb,
-                local=local, fwd=fwd, relay=relay, source=source, place=place)
+        taken.append(order)
+        windows.append(wins)
+    return dict(cores=cores, cnt=cnt, n=n, mine=mine, chipmates=chipmates, seq=seq, na=na, posa=posa, posb=posb, split=split,
+                local=local, fwd=fwd, relay=relay, source=source, direct=direct, union=union, place=place, taken=taken,
+                windows=windows)
 
 
 def rank_program(g, core, T, topo):
@@ -117,9 +238,7 @@ def rank_program(g, core, T, topo):
     total = sum(cnt[me])
     src = P["source"][me]
     place = P["place"][me]
-
-    seq, na = P["seq"][me], P["na"][me]
-    wa = max(na, LEAST)
+    seq, split = P["seq"][me], P["split"][me]
 
     def pieces(lo, hi):
         out, a = [], lo
@@ -132,19 +251,16 @@ def rank_program(g, core, T, topo):
     def load(q, a, b, sem):
         q.dma_start(T.xt[:, 4 * a:4 * b], T.x[:, 4 * seq[a]:4 * (seq[b - 1] + 1)]).then_inc(sem, 16)
 
-    first, rest = pieces(0, wa), pieces(wa, len(seq))
+    first, rest = pieces(0, split), pieces(split, len(seq))
     for i, (a, b) in enumerate(first):
         load([g.sync, g.scalar][i % 2], a, b, S.xa)
     for a, b in rest:
         load(g.sync, a, b, S.xb)
     g.sync.dma_start(T.wt[:, :], T.w[:, :]).then_inc(S.wl, 16)
 
-    lob, nb = P["lob"][me], P["nb"][me]
-    g.vector.wait_ge(S.xa, 16 * len(first))
-    g.vector.quantize_mx(T.qa[:, 0:wa], T.pa[:, 0:wa], T.xt[:, 0:4 * wa]).then_inc(S.qad, 1)
-    if rest:
-        g.vector.wait_ge(S.xb, 16 * len(rest))
-    g.vector.quantize_mx(T.qb[:, 0:nb], T.pb[:, 0:nb], T.xt[:, 4 * lob:4 * (lob + nb)]).then_inc(S.qbd, 1)
+    for a, b, loaded, k, done in ((0, split, S.xa, len(first), S.qad), (split, len(seq), S.xb, len(rest), S.qbd)):
+        g.vector.wait_ge(loaded, 16 * k)
+        g.vector.quantize_mx(T.q[:, a:b], T.p[:, a:b], T.xt[:, 4 * a:4 * b]).then_inc(done, 1)
     g.vector.wait_ge(S.wl, 16)
     g.vector.quantize_mx(T.qw[:, :], T.pw[:, :], T.wt[:, :]).then_inc(S.qwd, 1)
 
@@ -152,54 +268,57 @@ def rank_program(g, core, T, topo):
 
     def engines(sender, dests):
         here = cores[sender]
-        on = [e for e in dests if topo.host(cores[e]) == topo.host(here) and topo.chip(cores[e]) == topo.chip(here)]
-        off = [e for e in dests if e not in on]
+        on = [e for e in dests if e in P["chipmates"][sender]]
+        off = sorted(e for e in dests if e not in on)
         leave = bits(topo.mask(here, cores[P["relay"][sender]]))
         k = len(leave)
         while k * len(off) > len(leave):
             k //= 2
         out = {e: leave[i * k:(i + 1) * k] for i, e in enumerate(off)}
         for e in on:
-            out[e] = [i for i in bits(topo.mask(here, cores[e])) if i not in leave][::2]
+            out[e] = [i for i in bits(topo.mask(here, cores[e])) if i not in leave]
         assert len(on) <= 1
         return out
 
-    def send(buf, is_codes, need, w, base, limit, key, sem):
-        eng = engines(me, sorted(need))
-        tr = []
-        for e in sorted(need):
-            a = base + min(need[e][0], limit - w)
-            d = P["place"][e][key]
-            s_ap, d_ap = buf[:, a:a + w], (T.ql if is_codes else T.pl)[:, d:d + w]
-            if is_codes:
+    def send(buf, land, dests, key, sems, base=0):
+        eng, tr = engines(me, dests), []
+        for e in sorted(dests):
+            d, a, w = P["place"][e][key]
+            a += base
+            s_ap, d_ap = buf[:, a:a + w], land[:, d:d + w]
+            if land.name == T.ql.name:
                 s_ap, d_ap = s_ap.bitcast(dt.uint8), d_ap.bitcast(dt.uint8)
             rid, pid = topo.addr(cores[e], core)
-            tr.append(RemoteDMATransfer(dst_ids=[DstId(rid=rid, pnc=pid)], dma_engine_mask=as_mask(eng[e]), remote_sem=sem,
+            tr.append(RemoteDMATransfer(dst_ids=[DstId(rid=rid, pnc=pid)], dma_engine_mask=as_mask(eng[e]), remote_sem=sems[e],
                                         srcs=[s_ap], dsts=[d_ap]))
             sent[0] += len(eng[e])
         g.remote_dma_fused(tr, local_sem=S.sent)
 
     to = P["relay"][me]
-    rid, pid = topo.addr(cores[to], core)
-    hop_mask = topo.mask(core, cores[to])
-    d = P["place"][to]["hop"]
     g.wait_ge(S.qad, 1)
-    g.remote_dma(T.ql[:, d:d + na].bitcast(dt.uint8), T.qa[:, 0:na].bitcast(dt.uint8), S.hc, S.sent, pid, rid, hop_mask)
-    g.remote_dma(T.pl[:, d:d + na], T.pa[:, 0:na], S.hs, S.sent, pid, rid, hop_mask)
-    sent[0] += 2 * len(bits(hop_mask))
-
-    need, w = P["local"][me]
+    send(T.q, T.ql, [to], ("codes", me), {to: S.hop})
+    to = P["union"][me]
+    send(T.p, T.pl, to, ("plane", me), {e: S.direct for e in to})
+    to = P["local"][me]
     g.wait_ge(S.qbd, 1)
-    send(T.qb, True, need, w, 0, nb, ("local", me), S.loc)
-    send(T.pb, False, need, w, 0, nb, ("local", me), S.loc)
+    send(T.q, T.ql, to, ("local", me), {e: S.loc for e in to})
+    send(T.p, T.pl, to, ("local", me), {e: S.loc for e in to})
 
-    hop_inc = len(bits(topo.mask(cores[src], core)))
-    need, w = P["fwd"][src, me]
-    hop, hop_n = place["hop"], P["na"][src]
-    g.wait_ge(S.hc, hop_inc)
-    send(T.ql, True, need, w, hop, hop_n, ("relay", src), S.rel)
-    g.wait_ge(S.hs, hop_inc)
-    send(T.pl, False, need, w, hop, hop_n, ("relay", src), S.rel)
+    hop_inc = len(engines(src, [me])[me])
+    to = P["fwd"][src]
+    g.wait_ge(S.hop, hop_inc)
+    send(T.ql, T.ql, to, ("codes", src), {e: S["rel%d" % P["taken"][e].index(src)] for e in to}, place["base"][src])
+
+    direct_inc = sum(len(engines(j, P["union"][j])[me]) for j in P["direct"][me])
+    other = [r for r in P["chipmates"][me] if r != me][0]
+
+    def shared(r, to):
+        return [j for j in P["direct"][r] if to in P["fwd"][j] or P["source"][to] == j and span(P["posa"][j], [(to - 1) % n, to])]
+    if direct_inc:
+        g.wait_ge(S.direct, direct_inc)
+    for j in shared(me, other):
+        send(T.pl, T.pl, [other], ("plane", j), {other: S.shared}, place["base"][j])
+    shared_inc = len(shared(other, me)) * len(engines(other, [me])[me])
     g.wait_ge(S.sent, sent[0])
 
     prev = (me - 1) % n
@@ -210,72 +329,73 @@ def rank_program(g, core, T, topo):
             yat[half, j] = at
             at += cnt[j][f]
 
-    def runs(j, pos, shift):
-        return [(yat[half, j], shift + pos[f][0], cnt[j][f]) for half, f in enumerate((me, prev)) if cnt[j][f]]
+    def runs(j, pos, base):
+        return [(half, yat[half, j], base + pos[f][0], cnt[j][f]) for half, f in enumerate((me, prev)) if cnt[j][f]]
 
-    own = runs(me, P["posb"][me], 0)
-    loc, loc_inc = [], 0
+    def around(rs, a, b):
+        if not rs:
+            return None
+        lo, hi = min(r[2] for r in rs), max(r[2] + r[3] for r in rs)
+        lo = max(a, min(lo, hi - LEAST))
+        hi = max(hi, lo + LEAST)
+        assert hi <= b
+        return lo, hi
+
+    rs = runs(me, P["posb"][me], 0)
+    groups = [(T.q, T.p, rs, around(rs, 0, len(seq)), [(S.qad, 1), (S.qbd, 1), (S.qwd, 1)], "v", "e")]
+    rs, inc = [], 0
     for j in mine[me]:
         if ("local", j) in place:
-            nd, w = P["local"][j]
-            loc += runs(j, P["posb"][j], place["local", j] - min(nd[me][0], P["nb"][j] - w))
-            loc_inc += 2 * len(engines(j, sorted(nd))[me])
-    hopr = runs(src, P["posa"][src], hop)
-    rel, rel_inc = [], 0
-    for r in mine[me]:
-        j = P["source"][r]
-        if ("relay", j) in place:
-            nd, w = P["fwd"][j, r]
-            rel.append(runs(j, P["posa"][j], place["relay", j] - min(nd[me][0], P["na"][j] - w)))
-            rel_inc += 2 * len(engines(r, sorted(nd))[me])
+            d, a, _ = place["local", j]
+            rs += runs(j, P["posb"][j], d - a)
+            inc += 2 * len(engines(j, P["local"][j])[me])
+    groups.append((T.ql, T.pl, rs, around(rs, *place["loc"]), [(S.loc, inc)] if inc else [], "s", "e"))
+    wait = [(s, v) for s, v in ((S.hop, hop_inc), (S.direct, direct_inc), (S.shared, shared_inc)) if v]
+    picks = 0
+    for t, j in enumerate(P["taken"][me]):
+        rs = runs(j, P["posa"][j], place["base"][j])
+        if j != src:
+            wait.append((S["rel%d" % t], len(engines(P["relay"][j], P["fwd"][j])[me])))
+        found = [w for k, w in P["windows"][me].items() if k[0] == j]
+        if t < len(P["taken"][me]) - 1:
+            groups.append((T.ql, T.pl, rs, found[0] if rs else None, wait, "vs"[picks % 2], "l"))
+            picks += len(rs) > 0
+            wait = []
+        else:
+            for r, w in zip(rs, found):
+                groups.append((T.ql, T.pl, [r], w, wait, "vs"[r[0]], "l"))
+                wait = []
 
-    def work(rs):
-        return sum(max(c, 64) for x in rs for _, _, c in x)
-    k = min(range(len(rel) + 1), key=lambda k: max(work(rel[:k]), work(rel[k:])))
-    rel_v, rel_s = [x for y in rel[:k] for x in y], [x for y in rel[k:] for x in y]
+    for b, (q, p, rs, win, wait, eng, phase) in enumerate(groups):
+        for s, v in wait:
+            g.tensor.wait_ge(s, v)
+        if rs:
+            lo, hi = win
+            g.tensor.matmul_mx(T.ps[:, 512 * b:512 * b + hi - lo], T.qw[:, :], T.pw[:, :], q[:, lo:hi], p[:, lo:hi],
+                               True, True).then_inc(S["m%d" % b], 1)
 
-    groups = [(T.qb, T.pb, own, nb), (T.ql, T.pl, loc, hop), (T.ql, T.pl, hopr, hop + hop_n),
-              (T.ql, T.pl, rel_v, LAND), (T.ql, T.pl, rel_s, LAND)]
-    lows = []
-    for b, (q, p, rs, end) in enumerate(groups):
-        if b == 0:
-            g.tensor.wait_ge(S.qbd, 1)
-            g.tensor.wait_ge(S.qwd, 1)
-        elif b == 1 and loc_inc:
-            g.tensor.wait_ge(S.loc, loc_inc)
-        elif b == 2:
-            g.tensor.wait_ge(S.hc, hop_inc)
-            g.tensor.wait_ge(S.hs, hop_inc)
-        elif b == 3 and rel_inc:
-            g.tensor.wait_ge(S.rel, rel_inc)
-        lows.append(0)
-        if not rs:
-            continue
-        lo, hi = min(a for _, a, c in rs), max(a + c for _, a, c in rs)
-        lo = max(0, min(lo, hi - LEAST))
-        hi = max(hi, lo + LEAST)
-        assert hi <= end and hi - lo <= 512
-        lows[b] = lo
-        g.tensor.matmul_mx(T.ps[:, 512 * b:512 * b + hi - lo], T.qw[:, :], T.pw[:, :], q[:, lo:hi], p[:, lo:hi],
-                           True, True).then_inc(S["m%d" % b], 1)
+    copied = {}
 
     def pick(b):
-        rs = groups[b][2]
+        _, _, rs, win, _, eng, phase = groups[b]
         if not rs:
             return
-        q = g.scalar if b in (1, 4) else g.vector
+        q = g.vector if eng == "v" else g.scalar
         q.wait_ge(S["m%d" % b], 1)
-        for y, a, c in rs:
-            o, i = T.ys[:, y:y + c], T.ps[:, 512 * b + a - lows[b]:512 * b + a - lows[b] + c]
-            if b in (1, 4):
-                q.activation(o, i, ActivationFunctionType.Copy).then_inc(S["c%d" % b], 1)
+        for half, y, a, c in rs:
+            o, i = T.ys[:, y:y + c], T.ps[:, 512 * b + a - win[0]:512 * b + a - win[0] + c]
+            name = "c%s%d%s" % (phase, half, eng)
+            if eng == "v":
+                q.tensor_copy(o, i).then_inc(S[name], 1)
             else:
-                q.tensor_copy(o, i).then_inc(S["c%d" % b], 1)
+                q.activation(o, i, ActivationFunctionType.Copy).then_inc(S[name], 1)
+            copied[name] = copied.get(name, 0) + 1
 
-    def store(q, half, js, banks):
-        for b in banks:
-            if groups[b][2]:
-                q.wait_ge(S["c%d" % b], len(groups[b][2]))
+    def store(q, half, js, phase):
+        for eng in "vs":
+            name = "c%s%d%s" % (phase, half, eng)
+            if name in copied:
+                q.wait_ge(S[name], copied[name])
         lo = yat[half, js[0]]
         hi = yat[half, js[-1]] + cnt[js[-1]][(me, prev)[half]]
         if hi > lo:
@@ -284,13 +404,15 @@ def rank_program(g, core, T, topo):
         return 0
 
     far = [j for j in range(n) if j not in mine[me]]
-    pick(0)
-    pick(2)
-    pick(3)
+    for b, gr in enumerate(groups):
+        if gr[5] == "v":
+            pick(b)
     pick(1)
-    k = store(g.scalar, 1, mine[me], (0, 1))
-    pick(4)
-    k += store(g.scalar, 1, far, (2, 3, 4))
-    k += store(g.sync, 0, mine[me], (0, 1))
-    k += store(g.sync, 0, far, (2, 3, 4))
+    k = store(g.scalar, 1, mine[me], "e")
+    for b, gr in enumerate(groups):
+        if gr[5] == "s" and b != 1:
+            pick(b)
+    k += store(g.scalar, 1, far, "l")
+    k += store(g.sync, 0, mine[me], "e")
+    k += store(g.sync, 0, far, "l")
     g.sync.wait_ge(S.st, 16 * k)

from concourse.bass import DstId, RemoteDMATransfer
from concourse.mybir import dt, ActivationFunctionType

TILE, LAND = 512, 2048
SCRATCH = {
    "xt": ("sbuf", [128, 4 * TILE], "bfloat16"),
    "wt": ("sbuf", [128, 512], "bfloat16"),
    "q": ("sbuf", [128, TILE], "float8_e4m3fn_x4"),
    "p": ("sbuf", [128, TILE], "uint8"),
    "qw": ("sbuf", [128, 128], "float8_e4m3fn_x4"),
    "pw": ("sbuf", [128, 128], "uint8"),
    "ql": ("sbuf", [128, LAND], "float8_e4m3fn_x4"),
    "pl": ("sbuf", [128, LAND], "uint8"),
    "ys": ("sbuf", [128, 512], "float32"),
    "ps": ("psum", [128, 8 * 512], "float32"),
}
SEMAPHORES = (["xa", "xb", "wl", "qad", "qbd", "qwd", "sent", "hop", "direct", "shared", "loc", "st"] + ["rel%d" % i for i in range(8)]
              + ["m%d" % b for b in range(8)] + ["c%s%d%s" % (a, h, e) for a in "el" for h in (0, 1) for e in "vs"])
LEAST = 128


def bits(m):
    return [i for i in range(m.bit_length()) if m >> i & 1]


def as_mask(engines):
    return sum(1 << i for i in engines)


def span(pos, fs):
    r = sorted(pos[f] for f in fs if pos[f][1] > pos[f][0])
    if not r:
        return None
    assert all(a[1] == b[0] for a, b in zip(r, r[1:]))
    return r[0][0], r[-1][1]


def spans(pos, wants):
    need = {e: span(pos, fs) for e, fs in wants.items()}
    return {e: r for e, r in need.items() if r}


def positions(order, c, at=0):
    pos = {}
    for f in order:
        pos[f] = (at, at + c[f])
        at += c[f]
    return pos


def width(need):
    return max(b - a for a, b in need.values())


def both(x, y):
    return (max(x[0], y[0]), min(x[1], y[1]))


def orders(items):
    if not items:
        yield []
    for i, x in enumerate(items):
        for rest in orders(items[:i] + items[i + 1:]):
            yield [x] + rest


def arrange(nloc, items, seek, turn, hop):
    for order in orders(["local"] + sorted(items)):
        at, base, whole, loc = 0, {}, {}, 0
        for j in order:
            if j == "local":
                loc = at
                whole[j] = (at, at + nloc)
                at += nloc
            else:
                c, p = items[j]
                lo, hi = min(c[0], p[0]), max(c[1], p[1])
                base[j] = at - lo
                f = both(c, p)
                whole[j] = (base[j] + f[0], base[j] + max(f))
                at += hi - lo
        here, windows, taken, todo = {"local", hop}, {}, [], list(turn)

        def window(r, have):
            lo = hi = None
            for j in order:
                a, b = whole[j]
                if j in have and b > a:
                    lo, hi = (lo, b) if hi == a else (a, b)
                    if lo <= r[0] and r[1] <= hi:
                        end = hi
                        for i in order[order.index(j) + 1:]:
                            if i not in have or whole[i][0] != end or whole[i][1] == end:
                                break
                            end = whole[i][1]
                        if end - lo < LEAST:
                            return None
                        a = max(lo, min(r[0], r[1] - LEAST))
                        return a, max(r[1], a + LEAST)
            return None

        def take(j):
            got = [window((base[j] + r[0], base[j] + r[1]), here | {j}) for r in seek[j]]
            if None in got:
                return False
            here.add(j)
            taken.append(j)
            windows.update({(j, r): w for r, w in zip(seek[j], got)})
            return True

        ok, waiting = True, True
        while ok and (todo or waiting):
            if waiting and take(hop):
                waiting = False
            elif todo and not (waiting and len(todo) == 1):
                ok = take(todo.pop(0))
            else:
                ok = False
        if ok:
            return loc, base, at, taken, windows
    assert False, "no order of the sources gives every run a window"


def plan(T, topo):
    cores, cnt = list(T.cores), T.tables["CNT"]
    n = len(cores)
    mine = [[r for r in range(n) if topo.host(cores[r]) == topo.host(cores[j])] for j in range(n)]
    chipmates = [[r for r in mine[j] if topo.chip(cores[r]) == topo.chip(cores[j])] for j in range(n)]

    seq, na, posa, posb, split = [], [], [], [], []
    for j in range(n):
        s, h, c = mine[j][0], len(mine[j]), cnt[j]
        off = [sum(c[:f]) for f in range(n + 1)]
        far = [(s + h - 1 + i) % n for i in range(n - h + 1)]
        near = [(s - 1 + i) % n for i in range(h + 1)]
        q = [x for f in far + near[1:] for x in range(off[f], off[f + 1])]
        na.append(sum(c[f] for f in far))
        posa.append(positions(far, c))
        posb.append(positions(near, c, posa[j][near[0]][0]))
        split.append(max(na[j], LEAST))
        more = q[-1] + 1
        while len(q) < split[j] + LEAST:
            q.append(more % sum(c))
            more += 1
        seq.append(q)

    def wants(dests):
        return {e: [(e - 1) % n, e] for e in dests}

    local = [spans(posb[j], wants([e for e in mine[j] if e != j])) for j in range(n)]

    cand = [[r for r in range(n) if r not in mine[j] and topo.same_plane(cores[j], cores[r])] for j in range(n)]
    fwd = {(j, r): spans(posa[j], wants([e for e in mine[r] if e != r])) for j in range(n) for r in cand[j]}
    work = {(j, r): na[j] + width(v) * len([e for e in v if e not in chipmates[r]]) for (j, r), v in fwd.items()}
    relay = {}
    for group in sorted(set(tuple(m) for m in mine)):
        tried = []

        def search(k, chosen):
            if k == len(group):
                cost = [work[j, r] for j, r in chosen.items()]
                cross = sum(na[j] for j, r in chosen.items() if topo.die(cores[j]) != topo.die(cores[r]))
                tried.append(((max(cost), sum(cost), cross), sorted(chosen.items())))
                return
            for r in cand[group[k]]:
                if r not in chosen.values():
                    search(k + 1, {**chosen, group[k]: r})
        search(0, {})
        for j, r in min(tried)[1]:
            relay[j] = r
    source = {r: j for j, r in relay.items()}
    fwd = [fwd[j, relay[j]] for j in range(n)]
    work = [work[j, relay[j]] for j in range(n)]

    direct, union = [[] for _ in range(n)], [{} for _ in range(n)]
    for r in range(n):
        i = chipmates[r].index(r)
        for j in [j for j in range(n) if j not in mine[r]][i::len(chipmates[r])]:
            fs = sorted(set(f for e in chipmates[r] for f in ((e - 1) % n, e)))
            if span(posa[j], fs):
                union[j][r] = span(posa[j], fs)
                direct[r].append(j)

    place, taken, windows = [], [], []
    for e in range(n):
        at, p, items, seek = 0, {}, {}, {}
        for j in mine[e]:
            if e in local[j]:
                w = width(local[j])
                p["local", j] = (at, min(local[j][e][0], len(seq[j]) - w), w)
                at += w
        turn = sorted([source[r] for r in mine[e] if r != e and e in fwd[source[r]]], key=lambda j: (work[j], j))
        for r in chipmates[e]:
            for j in direct[r]:
                if r == e or e in fwd[j] or source[e] == j:
                    w = width(union[j])
                    a = min(union[j][r][0], na[j] - w)
                    items[j] = ((a, a), (a, a + w))
        for j in set(turn + [source[e]]):
            need = span(posa[j], [(e - 1) % n, e])
            planes = items[j][1] if j in items else (0, 0)
            if j == source[e]:
                codes = (0, na[j])
            else:
                w = width(fwd[j])
                starts = range(max(0, need[1] - w), min(need[0], na[j] - w) + 1, 2)
                a = max(starts, key=lambda a: (both((a, a + w), planes)[1] - both((a, a + w), planes)[0], a))
                codes = (a, a + w)
            items[j] = (codes, planes)
            if not need:
                seek[j] = []
            elif turn and j == turn[-1]:
                seek[j] = [posa[j][f] for f in (e, (e - 1) % n) if cnt[j][f]]
            else:
                seek[j] = [need]
        loc, base, end, order, wins = arrange(at, items, seek, turn, source[e])
        assert end <= LAND
        p = {k: (loc + d, a, w) for k, (d, a, w) in p.items()}
        for j, (codes, planes) in items.items():
            p["codes", j] = (base[j] + codes[0], codes[0], codes[1] - codes[0])
            p["plane", j] = (base[j] + planes[0], planes[0], planes[1] - planes[0])
        p["base"], p["loc"] = base, (loc, loc + at)
        place.append(p)
        taken.append(order)
        windows.append(wins)
    return dict(cores=cores, cnt=cnt, n=n, mine=mine, chipmates=chipmates, seq=seq, na=na, posa=posa, posb=posb, split=split,
                local=local, fwd=fwd, relay=relay, source=source, direct=direct, union=union, place=place, taken=taken,
                windows=windows)


def rank_program(g, core, T, topo):
    me = T.rank_of(core)
    if me is None:
        return
    P = plan(T, topo)
    cores, cnt, n, mine = P["cores"], P["cnt"], P["n"], P["mine"]
    S = T.sem
    total = sum(cnt[me])
    src = P["source"][me]
    place = P["place"][me]
    seq, split = P["seq"][me], P["split"][me]

    def pieces(lo, hi):
        out, a = [], lo
        for i in range(lo + 1, hi + 1):
            if i == hi or seq[i] != seq[i - 1] + 1:
                out.append((a, i))
                a = i
        return out

    def load(q, a, b, sem):
        q.dma_start(T.xt[:, 4 * a:4 * b], T.x[:, 4 * seq[a]:4 * (seq[b - 1] + 1)]).then_inc(sem, 16)

    first, rest = pieces(0, split), pieces(split, len(seq))
    for i, (a, b) in enumerate(first):
        load([g.sync, g.scalar][i % 2], a, b, S.xa)
    for a, b in rest:
        load(g.sync, a, b, S.xb)
    g.sync.dma_start(T.wt[:, :], T.w[:, :]).then_inc(S.wl, 16)

    for a, b, loaded, k, done in ((0, split, S.xa, len(first), S.qad), (split, len(seq), S.xb, len(rest), S.qbd)):
        g.vector.wait_ge(loaded, 16 * k)
        g.vector.quantize_mx(T.q[:, a:b], T.p[:, a:b], T.xt[:, 4 * a:4 * b]).then_inc(done, 1)
    g.vector.wait_ge(S.wl, 16)
    g.vector.quantize_mx(T.qw[:, :], T.pw[:, :], T.wt[:, :]).then_inc(S.qwd, 1)

    sent = [0]

    def engines(sender, dests):
        here = cores[sender]
        on = [e for e in dests if e in P["chipmates"][sender]]
        off = sorted(e for e in dests if e not in on)
        leave = bits(topo.mask(here, cores[P["relay"][sender]]))
        k = len(leave)
        while k * len(off) > len(leave):
            k //= 2
        out = {e: leave[i * k:(i + 1) * k] for i, e in enumerate(off)}
        for e in on:
            out[e] = [i for i in bits(topo.mask(here, cores[e])) if i not in leave]
        assert len(on) <= 1
        return out

    def send(buf, land, dests, key, sems, base=0):
        eng, tr = engines(me, dests), []
        for e in sorted(dests):
            d, a, w = P["place"][e][key]
            a += base
            s_ap, d_ap = buf[:, a:a + w], land[:, d:d + w]
            if land.name == T.ql.name:
                s_ap, d_ap = s_ap.bitcast(dt.uint8), d_ap.bitcast(dt.uint8)
            rid, pid = topo.addr(cores[e], core)
            tr.append(RemoteDMATransfer(dst_ids=[DstId(rid=rid, pnc=pid)], dma_engine_mask=as_mask(eng[e]), remote_sem=sems[e],
                                        srcs=[s_ap], dsts=[d_ap]))
            sent[0] += len(eng[e])
        g.remote_dma_fused(tr, local_sem=S.sent)

    to = P["relay"][me]
    g.wait_ge(S.qad, 1)
    send(T.q, T.ql, [to], ("codes", me), {to: S.hop})
    to = P["union"][me]
    send(T.p, T.pl, to, ("plane", me), {e: S.direct for e in to})
    to = P["local"][me]
    g.wait_ge(S.qbd, 1)
    send(T.q, T.ql, to, ("local", me), {e: S.loc for e in to})
    send(T.p, T.pl, to, ("local", me), {e: S.loc for e in to})

    hop_inc = len(engines(src, [me])[me])
    to = P["fwd"][src]
    g.wait_ge(S.hop, hop_inc)
    send(T.ql, T.ql, to, ("codes", src), {e: S["rel%d" % P["taken"][e].index(src)] for e in to}, place["base"][src])

    direct_inc = sum(len(engines(j, P["union"][j])[me]) for j in P["direct"][me])
    other = [r for r in P["chipmates"][me] if r != me][0]

    def shared(r, to):
        return [j for j in P["direct"][r] if to in P["fwd"][j] or P["source"][to] == j and span(P["posa"][j], [(to - 1) % n, to])]
    if direct_inc:
        g.wait_ge(S.direct, direct_inc)
    for j in shared(me, other):
        send(T.pl, T.pl, [other], ("plane", j), {other: S.shared}, place["base"][j])
    shared_inc = len(shared(other, me)) * len(engines(other, [me])[me])
    g.wait_ge(S.sent, sent[0])

    prev = (me - 1) % n
    yat = {}
    for half, f in enumerate((me, prev)):
        at = half * total
        for j in range(n):
            yat[half, j] = at
            at += cnt[j][f]

    def runs(j, pos, base):
        return [(half, yat[half, j], base + pos[f][0], cnt[j][f]) for half, f in enumerate((me, prev)) if cnt[j][f]]

    def around(rs, a, b):
        if not rs:
            return None
        lo, hi = min(r[2] for r in rs), max(r[2] + r[3] for r in rs)
        lo = max(a, min(lo, hi - LEAST))
        hi = max(hi, lo + LEAST)
        assert hi <= b
        return lo, hi

    rs = runs(me, P["posb"][me], 0)
    groups = [(T.q, T.p, rs, around(rs, 0, len(seq)), [(S.qad, 1), (S.qbd, 1), (S.qwd, 1)], "v", "e")]
    rs, inc = [], 0
    for j in mine[me]:
        if ("local", j) in place:
            d, a, _ = place["local", j]
            rs += runs(j, P["posb"][j], d - a)
            inc += 2 * len(engines(j, P["local"][j])[me])
    groups.append((T.ql, T.pl, rs, around(rs, *place["loc"]), [(S.loc, inc)] if inc else [], "s", "e"))
    wait = [(s, v) for s, v in ((S.hop, hop_inc), (S.direct, direct_inc), (S.shared, shared_inc)) if v]
    picks = 0
    for t, j in enumerate(P["taken"][me]):
        rs = runs(j, P["posa"][j], place["base"][j])
        if j != src:
            wait.append((S["rel%d" % t], len(engines(P["relay"][j], P["fwd"][j])[me])))
        found = [w for k, w in P["windows"][me].items() if k[0] == j]
        if t < len(P["taken"][me]) - 1:
            groups.append((T.ql, T.pl, rs, found[0] if rs else None, wait, "vs"[picks % 2], "l"))
            picks += len(rs) > 0
            wait = []
        else:
            for r, w in zip(rs, found):
                groups.append((T.ql, T.pl, [r], w, wait, "vs"[r[0]], "l"))
                wait = []

    for b, (q, p, rs, win, wait, eng, phase) in enumerate(groups):
        for s, v in wait:
            g.tensor.wait_ge(s, v)
        if rs:
            lo, hi = win
            g.tensor.matmul_mx(T.ps[:, 512 * b:512 * b + hi - lo], T.qw[:, :], T.pw[:, :], q[:, lo:hi], p[:, lo:hi],
                               True, True).then_inc(S["m%d" % b], 1)

    copied = {}

    def pick(b):
        _, _, rs, win, _, eng, phase = groups[b]
        if not rs:
            return
        q = g.vector if eng == "v" else g.scalar
        q.wait_ge(S["m%d" % b], 1)
        for half, y, a, c in rs:
            o, i = T.ys[:, y:y + c], T.ps[:, 512 * b + a - win[0]:512 * b + a - win[0] + c]
            name = "c%s%d%s" % (phase, half, eng)
            if eng == "v":
                q.tensor_copy(o, i).then_inc(S[name], 1)
            else:
                q.activation(o, i, ActivationFunctionType.Copy).then_inc(S[name], 1)
            copied[name] = copied.get(name, 0) + 1

    def store(q, half, js, phase):
        for eng in "vs":
            name = "c%s%d%s" % (phase, half, eng)
            if name in copied:
                q.wait_ge(S[name], copied[name])
        lo = yat[half, js[0]]
        hi = yat[half, js[-1]] + cnt[js[-1]][(me, prev)[half]]
        if hi > lo:
            q.dma_start(T.y[:, lo:hi], T.ys[:, lo:hi]).then_inc(S.st, 16)
            return 1
        return 0

    far = [j for j in range(n) if j not in mine[me]]
    for b, gr in enumerate(groups):
        if gr[5] == "v":
            pick(b)
    pick(1)
    k = store(g.scalar, 1, mine[me], "e")
    for b, gr in enumerate(groups):
        if gr[5] == "s" and b != 1:
            pick(b)
    k += store(g.scalar, 1, far, "l")
    k += store(g.sync, 0, mine[me], "e")
    k += store(g.sync, 0, far, "l")
    g.sync.wait_ge(S.st, 16 * k)
